import numpy as np
import ml_dtypes


def mxq(x, axis, fmt="e4m3"):
    dtype, down = {"e4m3": (ml_dtypes.float8_e4m3fn, 7), "e5m2": (ml_dtypes.float8_e5m2, 14)}[fmt]
    v = np.moveaxis(np.asarray(x, np.float32).astype(ml_dtypes.bfloat16).astype(np.float64), axis, -1)
    blocks = v.reshape(v.shape[:-1] + (-1, 32))
    amax = np.abs(blocks).max(-1, keepdims=True)
    byte = np.maximum(np.where(amax > 0, np.frexp(amax)[1] - 1 + 127, 0) - down, 1)
    scale = np.exp2(byte - 127.0)
    codes = (blocks / scale).astype(np.float32).astype(dtype).astype(np.float64)
    return np.moveaxis((codes * scale).reshape(v.shape), -1, axis)


WIDE = False


def mx_kscale(k):
    if not WIDE:
        return np.ones(k)
    levels = np.array([10, -10, 5, -5, 0])
    if k % 512:
        return np.exp2(np.random.permutation(np.resize(levels, k // 32))).repeat(32)
    a = np.empty((k // 512, 16))
    for p in range(k // 512):
        a[p, :8] = np.random.permutation(np.resize(levels, 8))
        for g in range(8):
            far = levels[np.abs(levels - a[p, g]) >= 10]
            a[p, g + 8] = far[np.random.randint(len(far))]
    return np.exp2(a.ravel()).repeat(32)


def f64(x):
    return np.asarray(x).astype(np.float64)


def striped(idx):
    return np.tile(np.asarray(idx).reshape(-1, 16).T, (8, 1)).astype(np.uint16)


def unstriped(offs):
    return offs[:16].T.reshape(-1).astype(np.int64)


E2M1 = np.array([0.0, 0.5, 1.0, 1.5, 2.0, 3.0, 4.0, 6.0, -0.0, -0.5, -1.0, -1.5, -2.0, -3.0, -4.0, -6.0])


def pack_weight(w, fmt):
    k, n = w.shape
    w = f64(np.asarray(w, np.float32).astype(ml_dtypes.bfloat16)).reshape(k // 32, 32, n)
    amax = np.abs(w).max(1)
    if fmt == "e4m3":
        byte = np.frexp(amax)[1] - 1 + 127 - 7
    else:
        mant, ex = np.frexp(amax / 6.0)
        byte = np.where(mant > 0.5, ex, ex - 1) + 127
    byte = np.clip(np.where(amax > 0, byte, 1), 1, 254)
    scaled = (w * np.exp2(127.0 - byte)[:, None, :]).reshape(k, n).astype(np.float32)
    by_word = np.ascontiguousarray(scaled.reshape(k // 512, 128, 4, n).transpose(0, 1, 3, 2))
    if fmt == "e4m3":
        words = by_word.astype(ml_dtypes.float8_e4m3fn).view(np.uint8)
    else:
        c = by_word.astype(ml_dtypes.float4_e2m1fn).view(np.uint8) & 0xF
        words = (c[..., 0::2] | (c[..., 1::2] << 4)).reshape(k // 512, 128, 2 * n)
    return np.ascontiguousarray(words), np.ascontiguousarray(byte.astype(np.uint8).reshape(k // 512, 16, n))


def unpack_weight(words, scales, fmt):
    g, _, n = scales.shape
    words = np.ascontiguousarray(words).reshape(g, 128, n, -1)
    if fmt == "e4m3":
        vals = words.view(ml_dtypes.float8_e4m3fn).astype(np.float64)
    else:
        nib = np.empty((g, 128, n, 4), np.uint8)
        nib[..., 0::2] = words & 0xF
        nib[..., 1::2] = words >> 4
        vals = E2M1[nib]
    vals = vals * np.repeat(np.exp2(scales.astype(np.float64) - 127.0), 8, axis=1)[..., None]
    return vals.transpose(0, 1, 3, 2).reshape(g * 512, n)


D, T, I, Q, E, G, M = 512, 2048, 512, 256, 512, 64, 1024


def setup_inputs():
    n = np.random.standard_normal
    idx = np.random.permutation(T)[:I]
    idx2 = np.random.permutation(M)[:Q]
    fd = mx_kscale(D)
    fi = mx_kscale(I)
    ti = np.ones(T)
    ti[idx] = fi
    keysp = pack_weight(n((D, T)) / fd[:, None], "e4m3")
    return {
        "query": (n((D, Q)) * 1.0 / np.sqrt(D) * fd[:, None]).astype(np.float32),
        "query2": (n((D, Q)) * 1.0 / np.sqrt(D) * fd[:, None]).astype(np.float32),
        "keys_words": keysp[0],
        "keys_scales": keysp[1],
        "prior1": np.tile(np.random.uniform(0.1, 0.9, T), (128, 1)).astype(np.float32),
        "lam": (np.random.uniform(0.7, 1.4, (Q, 1))).astype(np.float32),
        "cap": (np.random.uniform(0.01, 0.018, (Q, 1))).astype(np.float32),
        "os": (np.random.uniform(4.0, 16.0, (1, I)) * fi).astype(np.float32),
        "vals": (n((E, T)) / ti).astype(np.float32),
        "old": (n((E, M)) * 0.7).astype(np.float32),
        "offs": striped(idx),
        "offs2": striped(idx2),
    }


def reference(query, query2, keys_words, keys_scales, prior1, lam, cap, os, vals, old, offs, offs2):
    idx = unstriped(offs)
    idx2 = unstriped(offs2)
    keysu = unpack_weight(keys_words, keys_scales, "e4m3")
    queryq = mxq(f64(query), 0, "e4m3")
    keysidxg = keysu[:, idx]
    a = queryq.T @ keysidxg
    query2q = mxq(f64(query2), 0, "e4m3")
    b = query2q.T @ keysidxg
    ea = np.exp(a) * f64(prior1)[:1][:, idx]
    eb = np.exp(b) * (1.0 - f64(prior1)[:1][:, idx])
    s = np.log(ea + eb) * f64(lam)
    p = np.exp(s - np.max(s, axis=1, keepdims=True))
    r = p / np.sum(p, axis=1, keepdims=True)
    pg = r.reshape(Q, G, I // G).sum(axis=2)
    k0 = np.minimum(pg, f64(cap)) / pg
    kr = np.repeat(k0, I // G, axis=1)
    w = r * kr
    wo1 = w * f64(os)
    wt1 = wo1.T
    vt1 = f64(vals)[:, idx].T
    vt1q = mxq(vt1, 0, "e4m3")
    wt1q = mxq(wt1, 0, "e4m3")
    o = vt1q.T @ wt1q
    of = np.zeros((E, M))
    of[:, idx2] = o
    y = np.maximum(of, f64(old)) + f64(old) * 0.25
    return y

@@ -1,0 +1,319 @@
+from contextlib import ExitStack
+
+import concourse.mybir as mybir
+from concourse.masks import make_identity
+
+D, T, I, Q, E, G, M = 512, 2048, 512, 256, 512, 64, 1024
+P = 128
+PACK = 4
+RUN = I // G
+
+F32 = mybir.dt.float32
+BF16 = mybir.dt.bfloat16
+I32 = mybir.dt.int32
+U32 = mybir.dt.uint32
+U16 = mybir.dt.uint16
+U8 = mybir.dt.uint8
+FP8X4 = mybir.dt.float8_e4m3fn_x4
+ALU = mybir.AluOpType
+ACT = mybir.ActivationFunctionType
+AX = mybir.AxisListType
+
+FLOPS = 2 * (2 * D * Q * I + I * E * Q)
+BYTES = 4 * (2 * D * Q + T + 2 * Q + I + E * T + 2 * E * M) + D * T + (D // 32) * T + 2 * P * (I + Q) // 16
+
+
+def tile_attend_eitherquestion_runcap_keptlarger_kernel(
+    tc, query, query2, keys_words, keys_scales, prior1, lam, cap, slot_factor, vals, old, offs, offs2, out
+):
+    nc = tc.nc
+    slot_tiles = I // P
+    row_tiles = Q // P
+    feat_tiles = E // P
+
+    with ExitStack() as ctx:
+        sb = ctx.enter_context(tc.tile_pool(name="sb", bufs=1))
+        ps = ctx.enter_context(tc.psum_pool(name="ps", bufs=1))
+
+        def bank(b, shape, name):
+            return ps.tile(shape, F32, tag="bank%d" % b, name=name)
+
+        slots = sb.tile([P, I // 16], U16, name="slots")
+        places = sb.tile([P, Q // 16], U16, name="places")
+        scale_pool = sb.tile([P, T], U8, name="scale_pool", tag="stage1", align_bytes=64)
+        prior_pool = sb.tile([P, T], F32, name="prior_pool", tag="stage4", align_bytes=64)
+        key_pool = sb.tile([P, T], U32, name="key_pool", tag="stage2", align_bytes=64)
+        ident = sb.tile([P, P], F32, name="ident", align_bytes=64)
+        windows = [sb.tile([P, M], F32, name="window%d" % n, align_bytes=64) for n in range(2)]
+
+        nc.gpsimd.memset(scale_pool[:].bitcast(I32), 0)
+        nc.vector.memset(prior_pool[:], 0.0)
+        make_identity(nc, ident[:])
+        for n in range(2):
+            nc.vector.memset(windows[n][:], 0.0)
+
+        q_raw = [None, None]
+
+        def load_query(n):
+            q_raw[n] = sb.tile([P, PACK, Q], F32, name="q_raw%d" % n, tag="stage%d" % (3 * n), align_bytes=64)
+            nc.sync.dma_start(q_raw[n][:], (query, query2)[n].rearrange("(p t) q -> p t q", t=PACK))
+
+        val_pool = [None] * feat_tiles
+        old_sb = [None] * feat_tiles
+
+        def load_values(j):
+            val_pool[j] = sb.tile([P, T], F32, name="val_pool%d" % j, tag="stage%d" % j, align_bytes=64)
+            nc.sync.dma_start(val_pool[j][:], vals[j * P : (j + 1) * P, :])
+
+        def load_old(j):
+            old_sb[j] = sb.tile([P, M], F32, name="old_sb%d" % j, tag="stage%d" % j, align_bytes=64)
+            nc.sync.dma_start(old_sb[j][:], old[j * P : (j + 1) * P, :])
+
+        nc.sync.dma_start(slots[:], offs)
+        load_query(0)
+        for quad in range(4):
+            nc.scalar.dma_start(
+                scale_pool[32 * quad : 32 * quad + 4, :].bitcast(I32),
+                keys_scales[0, 4 * quad : 4 * quad + 4, :].bitcast(I32),
+            )
+        nc.sync.dma_start(key_pool[:].bitcast(I32), keys_words[0].rearrange("p n t -> p (n t)").bitcast(I32))
+        load_query(1)
+        nc.scalar.dma_start(prior_pool[0:1, :], prior1[0:1, :])
+        nc.sync.dma_start(places[:], offs2)
+
+        q_codes = [sb.tile([P, Q], U32, name="q_codes%d" % n, align_bytes=64) for n in range(2)]
+        q_scales = [sb.tile([P, Q], U8, name="q_scales%d" % n, align_bytes=64) for n in range(2)]
+
+        def quantise_query(n):
+            q_bf = sb.tile([P, Q, PACK], BF16, name="q_bf%d" % n, tag="small%d" % n, align_bytes=64)
+            nc.vector.tensor_copy(
+                q_bf[:].rearrange("p (c i) t -> p c t i", i=4),
+                q_raw[n][:].rearrange("p t (c i) -> p c t i", i=4),
+            )
+            nc.vector.quantize_mx(
+                out=q_codes[n][:].bitcast(FP8X4), scales=q_scales[n][:], in_=q_bf[:].rearrange("p q t -> p (q t)")
+            )
+
+        key_scales = sb.tile([P, I], U8, name="key_scales", align_bytes=64)
+        key_codes = sb.tile([P, I], U32, name="key_codes", align_bytes=64)
+        half = I // 2
+
+        quantise_query(0)
+        load_values(0)
+        nc.vector.tensor_copy(key_scales[:], scale_pool[:].indirect(slots[:]))
+        load_values(1)
+        for u in range(2):
+            nc.vector.tensor_copy(
+                key_codes[:, u * half : (u + 1) * half],
+                key_pool[:].indirect(slots[:, u * half // 16 : (u + 1) * half // 16]),
+            )
+
+        prior_row = sb.tile([P, I], F32, name="prior_row", tag="small2", align_bytes=64)
+        nc.scalar.activation(prior_row[:], prior_pool[:].indirect(slots[:]), ACT.Copy)
+        load_values(2)
+        lam_sb = sb.tile([P, row_tiles], F32, name="lam_sb", tag="small0", align_bytes=64)
+        with nc.allow_non_contiguous_dma(reason="one value a query row"):
+            nc.sync.dma_start(lam_sb[:], lam.rearrange("(h p) o -> p (h o)", p=P))
+        grown = [[None, None], [None, None]]
+
+        def score(n):
+            for u in range(2):
+                scores = bank(2 * n + u, [P, 2, Q], "scores%d%d" % (n, u))
+                for k in range(2):
+                    cols = slice((2 * u + k) * P, (2 * u + k + 1) * P)
+                    nc.tensor.matmul_mx(
+                        out=scores[:, k, :],
+                        lhsT=key_codes[:, cols].bitcast(FP8X4),
+                        lhsT_scale=key_scales[:, cols],
+                        rhs=q_codes[n][:].bitcast(FP8X4),
+                        rhs_scale=q_scales[n][:],
+                        start=True,
+                        stop=True,
+                    )
+                grown[n][u] = sb.tile([P, 2, Q], F32, name="grown%d%d" % (n, u), tag="grown%d%d" % (n, u), align_bytes=64)
+                nc.scalar.activation(grown[n][u][:], scores[:], ACT.Exp)
+
+        terms = [[None] * slot_tiles for n in range(2)]
+
+        def weigh(n):
+            for j in range(slot_tiles):
+                terms[n][j] = sb.tile([P, Q], F32, name="term%d%d" % (n, j), align_bytes=64)
+                nc.vector.tensor_scalar(
+                    terms[n][j][:], grown[n][j // 2][:, j % 2, :], prior[n][:, j : j + 1], None, ALU.mult
+                )
+
+        score(0)
+        quantise_query(1)
+        load_values(3)
+        factor_sb = sb.tile([P, PACK], F32, name="factor_sb", tag="small1", align_bytes=64)
+        nc.sync.dma_start(factor_sb[:], slot_factor.rearrange("o (p t) -> p (o t)", t=PACK))
+
+        prior_ps = bank(0, [P, slot_tiles, P], "prior_ps")
+        for j in range(slot_tiles):
+            nc.tensor.transpose(prior_ps[:, j, :], prior_row[:, j * P : (j + 1) * P], ident[:])
+        cap_sb = sb.tile([P, row_tiles], F32, name="cap_sb", tag="small2", align_bytes=64)
+        with nc.allow_non_contiguous_dma(reason="one value a query row"):
+            nc.sync.dma_start(cap_sb[:], cap.rearrange("(h p) o -> p (h o)", p=P))
+        prior = [sb.tile([P, slot_tiles], F32, name="prior%d" % n) for n in range(2)]
+        nc.vector.tensor_copy(prior[0][:], prior_ps[:, :, 0])
+        nc.vector.tensor_scalar(prior[1][:], prior_ps[:, :, 0], -1.0, 1.0, ALU.mult, ALU.add)
+        score(1)
+        weigh(0)
+        weigh(1)
+        clk1 = sb.tile([P, 1], F32, name="clk1")
+        nc.gpsimd.tensor_copy(clk1[:], terms[1][3][:, 0:1])
+
+        mix = [bank(4 + h, [P, I], "mix%d" % h) for h in range(row_tiles)]
+        for j in range(slot_tiles):
+            for h in range(row_tiles):
+                for n in range(2):
+                    nc.tensor.matmul(
+                        mix[h][:, j * P : (j + 1) * P],
+                        lhsT=terms[n][j][:, h * P : (h + 1) * P],
+                        rhs=ident[:],
+                        start=(n == 0),
+                        stop=(n == 1),
+                        is_transpose=True,
+                    )
+
+        neg_lam = sb.tile([P, row_tiles], F32, name="neg_lam")
+        nc.vector.tensor_scalar(neg_lam[:], lam_sb[:], -1.0, None, ALU.mult)
+
+        picked = [sb.tile([P, I], BF16, name="picked%d" % j, tag="grown1%d" % (1 - j), align_bytes=64) for j in range(2)]
+        v_codes = sb.tile([P, E], U32, name="v_codes", align_bytes=64)
+        v_scales = sb.tile([P, E], U8, name="v_scales", align_bytes=64)
+        v_turned = [None, None]
+        v_bf = [None, None]
+
+        def turn_values(c):
+            v_turned[c] = bank(6 + c, [P, 2, 2, P], "v_turned%d" % c)
+            for k in range(2):
+                words = picked[2 * c + k][:].bitcast(F32)
+                for u in range(2):
+                    nc.tensor.transpose(v_turned[c][:, k, u, :], words[:, u : I // 2 : 2], ident[:])
+            v_bf[c] = sb.tile([P, 2 * P * PACK], BF16, name="v_bf%d" % c, align_bytes=64)
+
+        def word_views(c):
+            return (
+                v_bf[c][:].bitcast(F32).rearrange("p (k e u) -> p k e u", k=2, u=2),
+                v_turned[c][:].rearrange("p k u e -> p k e u"),
+            )
+
+        def quantise_values(c):
+            cols = slice(c * 2 * P, (c + 1) * 2 * P)
+            nc.vector.quantize_mx(out=v_codes[:, cols].bitcast(FP8X4), scales=v_scales[:, cols], in_=v_bf[c][:])
+
+        for j in range(2):
+            nc.vector.tensor_copy(picked[j][:], val_pool[j][:].indirect(slots[:]))
+            load_old(j)
+
+        logs = [sb.tile([P, PACK, P], F32, name="logs%d" % h, align_bytes=64) for h in range(row_tiles)]
+        neg_s = [sb.tile([P, I], F32, name="neg_s%d" % h, tag="neg_s%d" % h, align_bytes=64) for h in range(row_tiles)]
+        neg_max = [sb.tile([P, 1], F32, name="neg_max%d" % h) for h in range(row_tiles)]
+        for h in range(row_tiles):
+            nc.scalar.activation(logs[h][:], mix[h][:].rearrange("p (s t) -> p t s", t=PACK), ACT.Ln)
+            nc.vector.tensor_scalar(
+                neg_s[h][:],
+                logs[h][:].rearrange("p t s -> p (t s)"),
+                neg_lam[:, h : h + 1],
+                None,
+                ALU.mult,
+                ALU.min,
+                accum_out=neg_max[h][:],
+            )
+
+        turn_values(0)
+        nc.vector.tensor_copy(*word_views(0))
+        quantise_values(0)
+
+        share = [sb.tile([P, I], F32, name="share%d" % h, align_bytes=64) for h in range(row_tiles)]
+        row_sum = [sb.tile([P, 1], F32, name="row_sum%d" % h) for h in range(row_tiles)]
+        cap_sum = [sb.tile([P, 1], F32, name="cap_sum%d" % h) for h in range(row_tiles)]
+        for h in range(row_tiles):
+            nc.scalar.activation(
+                share[h][:], neg_s[h][:], ACT.Exp, bias=neg_max[h][:], scale=-1.0, accum_out=row_sum[h][:]
+            )
+            nc.scalar.activation(cap_sum[h][:], row_sum[h][:], ACT.Copy, scale=cap_sb[:, h : h + 1])
+
+        run_sum = [sb.tile([P, G], F32, name="run_sum%d" % h) for h in range(row_tiles)]
+        clk2 = sb.tile([P, 1], F32, name="clk2")
+        nc.gpsimd.tensor_copy(clk2[:], share[0][:, 0:1])
+        bound = [sb.tile([P, G], F32, name="bound%d" % h) for h in range(row_tiles)]
+        inv_bound = [sb.tile([P, G], F32, name="inv_bound%d" % h) for h in range(row_tiles)]
+        run_factor = [sb.tile([P, G], F32, name="run_factor%d" % h) for h in range(row_tiles)]
+        weights = [sb.tile([P, PACK, P], F32, name="weights%d" % h, align_bytes=64) for h in range(row_tiles)]
+        for h in range(row_tiles):
+            nc.vector.tensor_reduce(
+                run_sum[h][:], share[h][:].rearrange("p (t g s) -> p g t s", t=PACK, g=G), AX.XY, ALU.add
+            )
+        for h in range(row_tiles):
+            nc.vector.tensor_scalar(bound[h][:], run_sum[h][:], cap_sum[h][:], None, ALU.max)
+        for h in range(row_tiles):
+            nc.vector.reciprocal(inv_bound[h][:], bound[h][:])
+        for h in range(row_tiles):
+            nc.vector.tensor_scalar(run_factor[h][:], inv_bound[h][:], cap_sb[:, h : h + 1], None, ALU.mult)
+        for h in range(row_tiles):
+            nc.vector.tensor_tensor(
+                weights[h][:].rearrange("p t (g s) -> p t g s", g=G),
+                share[h][:].rearrange("p (t g s) -> p t g s", t=PACK, g=G),
+                run_factor[h][:].rearrange("p (t g s) -> p t g s", t=1, s=1).to_broadcast([P, PACK, G, RUN // PACK]),
+                ALU.mult,
+            )
+
+        late_picked = sb.tile([P, 2, I], BF16, name="late_picked", tag="neg_s1", align_bytes=64)
+        picked = picked + [late_picked[:, 0, :], late_picked[:, 1, :]]
+        for j in range(2, 4):
+            nc.scalar.activation(picked[j][:], val_pool[j][:].indirect(slots[:]), ACT.Copy)
+            load_old(j)
+        turn_values(1)
+        nc.scalar.copy(*word_views(1))
+
+        w_codes = sb.tile([P, Q], U32, name="w_codes", align_bytes=64)
+        w_scales = sb.tile([P, Q], U8, name="w_scales", align_bytes=64)
+        w_bf = [sb.tile([P, P, PACK], BF16, name="w_bf%d" % h, align_bytes=64) for h in range(row_tiles)]
+        for h in range(row_tiles):
+            w_turned = bank(h, [P, PACK, P], "w_turned%d" % h)
+            for t in range(PACK):
+                nc.tensor.transpose(w_turned[:, t, :], weights[h][:, t, :], ident[:])
+            nc.vector.tensor_tensor(
+                w_bf[h][:],
+                w_turned[:].rearrange("p t q -> p q t"),
+                factor_sb[:].rearrange("p (q t) -> p q t", q=1).to_broadcast([P, P, PACK]),
+                ALU.mult,
+            )
+        for h in range(row_tiles):
+            cols = slice(h * P, (h + 1) * P)
+            nc.vector.quantize_mx(
+                out=w_codes[:, cols].bitcast(FP8X4), scales=w_scales[:, cols], in_=w_bf[h][:].rearrange("p q t -> p (q t)")
+            )
+        quantise_values(1)
+
+        for j in range(feat_tiles):
+            cols = slice(j * P, (j + 1) * P)
+            read = bank(2 + j, [P, Q], "read%d" % j)
+            nc.tensor.matmul_mx(
+                out=read[:],
+                lhsT=v_codes[:, cols].bitcast(FP8X4),
+                lhsT_scale=v_scales[:, cols],
+                rhs=w_codes[:].bitcast(FP8X4),
+                rhs_scale=w_scales[:],
+                start=True,
+                stop=True,
+            )
+            read_sb = sb.tile([P, Q], F32, name="read_sb%d" % j, align_bytes=64)
+            nc.scalar.copy(read_sb[:], read[:])
+            window = windows[j % 2]
+            nc.scalar.activation(window[:].indirect(places[:]), read_sb[:], ACT.Copy)
+            larger = sb.tile([P, M], F32, name="larger%d" % j, align_bytes=64)
+            result = sb.tile([P, M], F32, name="result%d" % j, align_bytes=64)
+            halves = [slice(0, M // 2), slice(M // 2, M)]
+            for cols in halves:
+                nc.vector.tensor_tensor(larger[:, cols], window[:, cols], old_sb[j][:, cols], ALU.max)
+            for cols in halves:
+                nc.vector.scalar_tensor_tensor(
+                    result[:, cols], old_sb[j][:, cols], 0.25, larger[:, cols], ALU.mult, ALU.add
+                )
+                if j == feat_tiles - 1:
+                    nc.sync.dma_start(out[j * P : (j + 1) * P, cols], result[:, cols])
+            if j < feat_tiles - 1:
+                nc.sync.dma_start(out[j * P : (j + 1) * P, :], result[:])

@@ -7,6 +7,7 @@ D, T, I, Q, E, G, M = 512, 2048, 512, 256, 512, 64, 1024
 P = 128
 PACK = 4
 RUN = I // G
+QUAD = 32
 
 F32 = mybir.dt.float32
 BF16 = mybir.dt.bfloat16
@@ -38,210 +39,201 @@ def tile_attend_eitherquestion_runcap_keptlarger_kernel(
         def bank(b, shape, name):
             return ps.tile(shape, F32, tag="bank%d" % b, name=name)
 
+        def tile(shape, dtype, name, buffer=None):
+            return sb.tile(shape, dtype, name=name, tag=buffer or name, align_bytes=64)
+
         slots = sb.tile([P, I // 16], U16, name="slots")
         places = sb.tile([P, Q // 16], U16, name="places")
-        scale_pool = sb.tile([P, T], U8, name="scale_pool", tag="stage1", align_bytes=64)
-        prior_pool = sb.tile([P, T], F32, name="prior_pool", tag="stage4", align_bytes=64)
-        key_pool = sb.tile([P, T], U32, name="key_pool", tag="stage2", align_bytes=64)
-        ident = sb.tile([P, P], F32, name="ident", align_bytes=64)
-        windows = [sb.tile([P, M], F32, name="window%d" % n, align_bytes=64) for n in range(2)]
+        scale_pool = tile([P, T], U8, "scale_pool")
+        prior_pool = tile([P, T], F32, "prior_pool")
+        key_pool = tile([P, T], U32, "key_pool")
+        q_raw = [tile([P, PACK, Q], F32, "q_raw%d" % n) for n in range(2)]
+        ident = tile([P, P], F32, "ident")
 
         nc.gpsimd.memset(scale_pool[:].bitcast(I32), 0)
-        nc.vector.memset(prior_pool[:], 0.0)
+        nc.vector.memset(prior_pool[:].bitcast(I32), 0)
         make_identity(nc, ident[:])
+        windows = [tile([P, M], F32, "window%d" % n) for n in range(2)]
         for n in range(2):
             nc.vector.memset(windows[n][:], 0.0)
 
-        q_raw = [None, None]
-
-        def load_query(n):
-            q_raw[n] = sb.tile([P, PACK, Q], F32, name="q_raw%d" % n, tag="stage%d" % (3 * n), align_bytes=64)
+        nc.sync.dma_start(slots[:], offs)
+        nc.sync.dma_start(places[:], offs2)
+        for n in range(2):
             nc.sync.dma_start(q_raw[n][:], (query, query2)[n].rearrange("(p t) q -> p t q", t=PACK))
+        for quad in range(P // QUAD):
+            nc.scalar.dma_start(
+                scale_pool[QUAD * quad : QUAD * quad + 4, :].bitcast(I32),
+                keys_scales[0, 4 * quad : 4 * quad + 4, :].bitcast(I32),
+            )
+        nc.scalar.dma_start(prior_pool[0:1, :], prior1[0:1, :])
+        nc.sync.dma_start(key_pool[:].bitcast(I32), keys_words[0].rearrange("p n t -> p (n t)").bitcast(I32))
 
         val_pool = [None] * feat_tiles
         old_sb = [None] * feat_tiles
 
-        def load_values(j):
-            val_pool[j] = sb.tile([P, T], F32, name="val_pool%d" % j, tag="stage%d" % j, align_bytes=64)
+        def load_values(j, buffer):
+            val_pool[j] = tile([P, T], F32, "val_pool%d" % j, buffer)
             nc.sync.dma_start(val_pool[j][:], vals[j * P : (j + 1) * P, :])
 
-        def load_old(j):
-            old_sb[j] = sb.tile([P, M], F32, name="old_sb%d" % j, tag="stage%d" % j, align_bytes=64)
+        def load_old(j, buffer):
+            old_sb[j] = tile([P, M], F32, "old_sb%d" % j, buffer)
             nc.sync.dma_start(old_sb[j][:], old[j * P : (j + 1) * P, :])
 
-        nc.sync.dma_start(slots[:], offs)
-        load_query(0)
-        for quad in range(4):
-            nc.scalar.dma_start(
-                scale_pool[32 * quad : 32 * quad + 4, :].bitcast(I32),
-                keys_scales[0, 4 * quad : 4 * quad + 4, :].bitcast(I32),
-            )
-        nc.sync.dma_start(key_pool[:].bitcast(I32), keys_words[0].rearrange("p n t -> p (n t)").bitcast(I32))
-        load_query(1)
-        nc.scalar.dma_start(prior_pool[0:1, :], prior1[0:1, :])
-        nc.sync.dma_start(places[:], offs2)
-
-        q_codes = [sb.tile([P, Q], U32, name="q_codes%d" % n, align_bytes=64) for n in range(2)]
-        q_scales = [sb.tile([P, Q], U8, name="q_scales%d" % n, align_bytes=64) for n in range(2)]
-
-        def quantise_query(n):
-            q_bf = sb.tile([P, Q, PACK], BF16, name="q_bf%d" % n, tag="small%d" % n, align_bytes=64)
+        q_codes = tile([P, 2, Q], U32, "q_codes")
+        q_scales = tile([P, 2, Q], U8, "q_scales")
+        for n in range(2):
+            q_bf = tile([P, Q, PACK], BF16, "q_bf%d" % n)
             nc.vector.tensor_copy(
                 q_bf[:].rearrange("p (c i) t -> p c t i", i=4),
                 q_raw[n][:].rearrange("p t (c i) -> p c t i", i=4),
             )
             nc.vector.quantize_mx(
-                out=q_codes[n][:].bitcast(FP8X4), scales=q_scales[n][:], in_=q_bf[:].rearrange("p q t -> p (q t)")
+                out=q_codes[:, n, :].bitcast(FP8X4), scales=q_scales[:, n, :], in_=q_bf[:].rearrange("p q t -> p (q t)")
             )
 
-        key_scales = sb.tile([P, I], U8, name="key_scales", align_bytes=64)
-        key_codes = sb.tile([P, I], U32, name="key_codes", align_bytes=64)
+        key_scales = tile([P, I], U8, "key_scales")
+        key_codes = [tile([P, P], U32, "key_codes%d" % j) for j in range(slot_tiles)]
         half = I // 2
 
-        quantise_query(0)
-        load_values(0)
-        nc.vector.tensor_copy(key_scales[:], scale_pool[:].indirect(slots[:]))
-        load_values(1)
-        for u in range(2):
-            nc.vector.tensor_copy(
-                key_codes[:, u * half : (u + 1) * half],
-                key_pool[:].indirect(slots[:, u * half // 16 : (u + 1) * half // 16]),
-            )
-
-        prior_row = sb.tile([P, I], F32, name="prior_row", tag="small2", align_bytes=64)
+        prior_row = tile([P, I], F32, "prior_row")
         nc.scalar.activation(prior_row[:], prior_pool[:].indirect(slots[:]), ACT.Copy)
-        load_values(2)
-        lam_sb = sb.tile([P, row_tiles], F32, name="lam_sb", tag="small0", align_bytes=64)
-        with nc.allow_non_contiguous_dma(reason="one value a query row"):
-            nc.sync.dma_start(lam_sb[:], lam.rearrange("(h p) o -> p (h o)", p=P))
-        grown = [[None, None], [None, None]]
-
-        def score(n):
-            for u in range(2):
-                scores = bank(2 * n + u, [P, 2, Q], "scores%d%d" % (n, u))
-                for k in range(2):
-                    cols = slice((2 * u + k) * P, (2 * u + k + 1) * P)
-                    nc.tensor.matmul_mx(
-                        out=scores[:, k, :],
-                        lhsT=key_codes[:, cols].bitcast(FP8X4),
-                        lhsT_scale=key_scales[:, cols],
-                        rhs=q_codes[n][:].bitcast(FP8X4),
-                        rhs_scale=q_scales[n][:],
-                        start=True,
-                        stop=True,
-                    )
-                grown[n][u] = sb.tile([P, 2, Q], F32, name="grown%d%d" % (n, u), tag="grown%d%d" % (n, u), align_bytes=64)
-                nc.scalar.activation(grown[n][u][:], scores[:], ACT.Exp)
-
-        terms = [[None] * slot_tiles for n in range(2)]
-
-        def weigh(n):
-            for j in range(slot_tiles):
-                terms[n][j] = sb.tile([P, Q], F32, name="term%d%d" % (n, j), align_bytes=64)
-                nc.vector.tensor_scalar(
-                    terms[n][j][:], grown[n][j // 2][:, j % 2, :], prior[n][:, j : j + 1], None, ALU.mult
-                )
-
-        score(0)
-        quantise_query(1)
-        load_values(3)
-        factor_sb = sb.tile([P, PACK], F32, name="factor_sb", tag="small1", align_bytes=64)
-        nc.sync.dma_start(factor_sb[:], slot_factor.rearrange("o (p t) -> p (o t)", t=PACK))
-
-        prior_ps = bank(0, [P, slot_tiles, P], "prior_ps")
+        prior_ps = bank(7, [P, slot_tiles, P], "prior_ps")
         for j in range(slot_tiles):
             nc.tensor.transpose(prior_ps[:, j, :], prior_row[:, j * P : (j + 1) * P], ident[:])
-        cap_sb = sb.tile([P, row_tiles], F32, name="cap_sb", tag="small2", align_bytes=64)
-        with nc.allow_non_contiguous_dma(reason="one value a query row"):
-            nc.sync.dma_start(cap_sb[:], cap.rearrange("(h p) o -> p (h o)", p=P))
-        prior = [sb.tile([P, slot_tiles], F32, name="prior%d" % n) for n in range(2)]
+        row_values = tile([P, P], F32, "row_values", "prior_pool")
+        nc.gpsimd.memset(row_values[:], 0.0)
+        nc.sync.dma_start(row_values[0:row_tiles, :], lam.rearrange("(h p) o -> h (p o)", p=P))
+        nc.sync.dma_start(row_values[QUAD : QUAD + row_tiles, :], cap.rearrange("(h p) o -> h (p o)", p=P))
+
+        nc.vector.tensor_copy(key_scales[:], scale_pool[:].indirect(slots[:]))
+        load_values(0, "q_raw1")
+        load_values(1, "scale_pool")
+        grown = [tile([P, 2, Q], F32, "grown%d" % j) for j in range(slot_tiles)]
+        for j in range(slot_tiles):
+            nc.vector.tensor_copy(key_codes[j][:], key_pool[:].indirect(slots[:, j * P // 16 : (j + 1) * P // 16]))
+            scores = bank(j, [P, 2 * Q], "scores%d" % j)
+            nc.tensor.matmul_mx(
+                out=scores[:],
+                lhsT=key_codes[j][:].bitcast(FP8X4),
+                lhsT_scale=key_scales[:, j * P : (j + 1) * P],
+                rhs=q_codes[:].rearrange("p n q -> p (n q)").bitcast(FP8X4),
+                rhs_scale=q_scales[:].rearrange("p n q -> p (n q)"),
+                start=True,
+                stop=True,
+            )
+            nc.scalar.activation(grown[j][:].rearrange("p n q -> p (n q)"), scores[:], ACT.Exp)
+        load_values(2, "key_pool")
+
+        prior = [tile([P, slot_tiles], F32, "prior%d" % n) for n in range(2)]
         nc.vector.tensor_copy(prior[0][:], prior_ps[:, :, 0])
         nc.vector.tensor_scalar(prior[1][:], prior_ps[:, :, 0], -1.0, 1.0, ALU.mult, ALU.add)
-        score(1)
-        weigh(0)
-        weigh(1)
-        clk1 = sb.tile([P, 1], F32, name="clk1")
-        nc.gpsimd.tensor_copy(clk1[:], terms[1][3][:, 0:1])
 
-        mix = [bank(4 + h, [P, I], "mix%d" % h) for h in range(row_tiles)]
+        mix_banks = [[4, 6], [5, 0]]
+        mix = [[bank(mix_banks[h][u], [P, half], "mix%d%d" % (h, u)) for u in range(2)] for h in range(row_tiles)]
         for j in range(slot_tiles):
+            terms = [tile([P, Q], F32, "term%d%d" % (j, n)) for n in range(2)]
+            for n in range(2):
+                nc.vector.tensor_scalar(terms[n][:], grown[j][:, n, :], prior[n][:, j : j + 1], None, ALU.mult)
             for h in range(row_tiles):
                 for n in range(2):
                     nc.tensor.matmul(
-                        mix[h][:, j * P : (j + 1) * P],
-                        lhsT=terms[n][j][:, h * P : (h + 1) * P],
+                        mix[h][j // 2][:, j % 2 * P : (j % 2 + 1) * P],
+                        lhsT=terms[n][:, h * P : (h + 1) * P],
                         rhs=ident[:],
                         start=(n == 0),
                         stop=(n == 1),
                         is_transpose=True,
                     )
+        factor_sb = tile([P, PACK], F32, "factor_sb", "grown0")
+        nc.sync.dma_start(factor_sb[:], slot_factor.rearrange("o (p t) -> p (o t)", t=PACK))
+        load_values(3, "term00")
 
-        neg_lam = sb.tile([P, row_tiles], F32, name="neg_lam")
-        nc.vector.tensor_scalar(neg_lam[:], lam_sb[:], -1.0, None, ALU.mult)
 
-        picked = [sb.tile([P, I], BF16, name="picked%d" % j, tag="grown1%d" % (1 - j), align_bytes=64) for j in range(2)]
-        v_codes = sb.tile([P, E], U32, name="v_codes", align_bytes=64)
-        v_scales = sb.tile([P, E], U8, name="v_scales", align_bytes=64)
-        v_turned = [None, None]
-        v_bf = [None, None]
+        v_codes = [None] * feat_tiles
+        v_scales = [None] * feat_tiles
+        picked = [None] * feat_tiles
 
-        def turn_values(c):
-            v_turned[c] = bank(6 + c, [P, 2, 2, P], "v_turned%d" % c)
-            for k in range(2):
-                words = picked[2 * c + k][:].bitcast(F32)
-                for u in range(2):
-                    nc.tensor.transpose(v_turned[c][:, k, u, :], words[:, u : I // 2 : 2], ident[:])
-            v_bf[c] = sb.tile([P, 2 * P * PACK], BF16, name="v_bf%d" % c, align_bytes=64)
-
-        def word_views(c):
-            return (
-                v_bf[c][:].bitcast(F32).rearrange("p (k e u) -> p k e u", k=2, u=2),
-                v_turned[c][:].rearrange("p k u e -> p k e u"),
-            )
-
-        def quantise_values(c):
-            cols = slice(c * 2 * P, (c + 1) * 2 * P)
-            nc.vector.quantize_mx(out=v_codes[:, cols].bitcast(FP8X4), scales=v_scales[:, cols], in_=v_bf[c][:])
-
-        for j in range(2):
+        def pick_values(j, buffer):
+            picked[j] = tile([P, I], BF16, "picked%d" % j, buffer)
             nc.vector.tensor_copy(picked[j][:], val_pool[j][:].indirect(slots[:]))
-            load_old(j)
 
-        logs = [sb.tile([P, PACK, P], F32, name="logs%d" % h, align_bytes=64) for h in range(row_tiles)]
-        neg_s = [sb.tile([P, I], F32, name="neg_s%d" % h, tag="neg_s%d" % h, align_bytes=64) for h in range(row_tiles)]
-        neg_max = [sb.tile([P, 1], F32, name="neg_max%d" % h) for h in range(row_tiles)]
+        def turn_values(first, count, b, bf_buffer, code_buffer):
+            v_turned = bank(b, [P, count, 2, P], "v_turned%d" % first)
+            for k in range(count):
+                words = picked[first + k][:].bitcast(F32)
+                for u in range(2):
+                    nc.tensor.transpose(v_turned[:, k, u, :], words[:, u : I // 2 : 2], ident[:])
+            v_bf = tile([P, count * P * PACK], BF16, "v_bf%d" % first, bf_buffer)
+            nc.scalar.copy(
+                v_bf[:].bitcast(F32).rearrange("p (k e u) -> p k e u", k=count, u=2),
+                v_turned[:].rearrange("p k u e -> p k e u"),
+            )
+            codes = tile([P, count * P], U32, "v_codes%d" % first, code_buffer)
+            scales = tile([P, count * P], U8, "v_scales%d" % first)
+            nc.vector.quantize_mx(out=codes[:].bitcast(FP8X4), scales=scales[:], in_=v_bf[:])
+            for k in range(count):
+                v_codes[first + k] = codes[:, k * P : (k + 1) * P]
+                v_scales[first + k] = scales[:, k * P : (k + 1) * P]
+
+        pick_values(0, "grown3")
+        load_old(0, "q_raw1")
+        pick_values(1, "term31")
+        load_old(1, "scale_pool")
+
+        cap_sb = tile([P, row_tiles], F32, "cap_sb")
+        logs = [tile([P, PACK, P], F32, "logs%d" % h) for h in range(row_tiles)]
+        slot_score = [tile([P, I], F32, "slot_score%d" % h) for h in range(row_tiles)]
+        row_max = [tile([P, 1], F32, "row_max%d" % h) for h in range(row_tiles)]
+        neg_max = [tile([P, 1], F32, "neg_max%d" % h) for h in range(row_tiles)]
         for h in range(row_tiles):
-            nc.scalar.activation(logs[h][:], mix[h][:].rearrange("p (s t) -> p t s", t=PACK), ACT.Ln)
+            for u in range(2):
+                nc.scalar.activation(
+                    logs[h][:, :, u * P // 2 : (u + 1) * P // 2],
+                    mix[h][u][:].rearrange("p (s t) -> p t s", t=PACK),
+                    ACT.Ln,
+                )
+                if h == 0 and u == 0:
+                    row_turned = bank(4, [P, P], "row_turned")
+                    nc.tensor.transpose(row_turned[:], row_values[:], ident[:])
             nc.vector.tensor_scalar(
-                neg_s[h][:],
+                slot_score[h][:],
                 logs[h][:].rearrange("p t s -> p (t s)"),
-                neg_lam[:, h : h + 1],
+                row_turned[:, h : h + 1],
                 None,
                 ALU.mult,
-                ALU.min,
-                accum_out=neg_max[h][:],
+                ALU.max,
+                accum_out=row_max[h][:],
             )
+            if h == 0:
+                nc.vector.tensor_copy(cap_sb[:], row_turned[:, QUAD : QUAD + row_tiles])
+            nc.vector.tensor_scalar(neg_max[h][:], row_max[h][:], -1.0, None, ALU.mult)
+        load_old(2, "logs0")
+        pick_values(2, "logs1")
+        load_old(3, "key_pool")
 
-        turn_values(0)
-        nc.vector.tensor_copy(*word_views(0))
-        quantise_values(0)
-
-        share = [sb.tile([P, I], F32, name="share%d" % h, align_bytes=64) for h in range(row_tiles)]
-        row_sum = [sb.tile([P, 1], F32, name="row_sum%d" % h) for h in range(row_tiles)]
-        cap_sum = [sb.tile([P, 1], F32, name="cap_sum%d" % h) for h in range(row_tiles)]
+        share = [tile([P, I], F32, "share%d" % h) for h in range(row_tiles)]
+        row_sum = [tile([P, 1], F32, "row_sum%d" % h) for h in range(row_tiles)]
+        cap_sum = [tile([P, 1], F32, "cap_sum%d" % h) for h in range(row_tiles)]
         for h in range(row_tiles):
             nc.scalar.activation(
-                share[h][:], neg_s[h][:], ACT.Exp, bias=neg_max[h][:], scale=-1.0, accum_out=row_sum[h][:]
+                share[h][:], slot_score[h][:], ACT.Exp, bias=neg_max[h][:], accum_out=row_sum[h][:]
             )
             nc.scalar.activation(cap_sum[h][:], row_sum[h][:], ACT.Copy, scale=cap_sb[:, h : h + 1])
 
-        run_sum = [sb.tile([P, G], F32, name="run_sum%d" % h) for h in range(row_tiles)]
-        clk2 = sb.tile([P, 1], F32, name="clk2")
-        nc.gpsimd.tensor_copy(clk2[:], share[0][:, 0:1])
-        bound = [sb.tile([P, G], F32, name="bound%d" % h) for h in range(row_tiles)]
-        inv_bound = [sb.tile([P, G], F32, name="inv_bound%d" % h) for h in range(row_tiles)]
-        run_factor = [sb.tile([P, G], F32, name="run_factor%d" % h) for h in range(row_tiles)]
-        weights = [sb.tile([P, PACK, P], F32, name="weights%d" % h, align_bytes=64) for h in range(row_tiles)]
+        turn_values(0, 2, 7, "slot_score1", None)
+        scaled = [tile([P, PACK, P], F32, "scaled%d" % h) for h in range(row_tiles)]
+        for h in range(row_tiles):
+            share_turned = bank(1 + h, [P, PACK, P], "share_turned%d" % h)
+            for t in range(PACK):
+                nc.tensor.transpose(share_turned[:, t, :], share[h][:, t * P : (t + 1) * P], ident[:])
+            for t in range(PACK):
+                nc.scalar.activation(scaled[h][:, t, :], share_turned[:, t, :], ACT.Copy, scale=factor_sb[:, t : t + 1])
+
+        run_sum = [tile([P, G], F32, "run_sum%d" % h) for h in range(row_tiles)]
+        bound = [tile([P, G], F32, "bound%d" % h) for h in range(row_tiles)]
+        inv_bound = [tile([P, G], F32, "inv_bound%d" % h) for h in range(row_tiles)]
+        run_factor = [tile([P, P], F32, "run_factor%d" % h) for h in range(row_tiles)]
         for h in range(row_tiles):
             nc.vector.tensor_reduce(
                 run_sum[h][:], share[h][:].rearrange("p (t g s) -> p g t s", t=PACK, g=G), AX.XY, ALU.add
@@ -251,34 +243,25 @@ def tile_attend_eitherquestion_runcap_keptlarger_kernel(
         for h in range(row_tiles):
             nc.vector.reciprocal(inv_bound[h][:], bound[h][:])
         for h in range(row_tiles):
-            nc.vector.tensor_scalar(run_factor[h][:], inv_bound[h][:], cap_sb[:, h : h + 1], None, ALU.mult)
-        for h in range(row_tiles):
-            nc.vector.tensor_tensor(
-                weights[h][:].rearrange("p t (g s) -> p t g s", g=G),
-                share[h][:].rearrange("p (t g s) -> p t g s", t=PACK, g=G),
-                run_factor[h][:].rearrange("p (t g s) -> p t g s", t=1, s=1).to_broadcast([P, PACK, G, RUN // PACK]),
+            nc.vector.tensor_scalar(
+                run_factor[h][:].rearrange("p (g s) -> p g s", g=G),
+                inv_bound[h][:].rearrange("p (g s) -> p g s", s=1).to_broadcast([P, G, RUN // PACK]),
+                cap_sb[:, h : h + 1],
+                None,
                 ALU.mult,
             )
 
-        late_picked = sb.tile([P, 2, I], BF16, name="late_picked", tag="neg_s1", align_bytes=64)
-        picked = picked + [late_picked[:, 0, :], late_picked[:, 1, :]]
-        for j in range(2, 4):
-            nc.scalar.activation(picked[j][:], val_pool[j][:].indirect(slots[:]), ACT.Copy)
-            load_old(j)
-        turn_values(1)
-        nc.scalar.copy(*word_views(1))
 
-        w_codes = sb.tile([P, Q], U32, name="w_codes", align_bytes=64)
-        w_scales = sb.tile([P, Q], U8, name="w_scales", align_bytes=64)
-        w_bf = [sb.tile([P, P, PACK], BF16, name="w_bf%d" % h, align_bytes=64) for h in range(row_tiles)]
+        w_codes = tile([P, Q], U32, "w_codes")
+        w_scales = tile([P, Q], U8, "w_scales")
+        w_bf = [tile([P, P, PACK], BF16, "w_bf%d" % h) for h in range(row_tiles)]
         for h in range(row_tiles):
-            w_turned = bank(h, [P, PACK, P], "w_turned%d" % h)
-            for t in range(PACK):
-                nc.tensor.transpose(w_turned[:, t, :], weights[h][:, t, :], ident[:])
+            factor_turned = bank(3 + h, [P, P], "factor_turned%d" % h)
+            nc.tensor.transpose(factor_turned[:], run_factor[h][:], ident[:])
             nc.vector.tensor_tensor(
                 w_bf[h][:],
-                w_turned[:].rearrange("p t q -> p q t"),
-                factor_sb[:].rearrange("p (q t) -> p q t", q=1).to_broadcast([P, P, PACK]),
+                scaled[h][:].rearrange("p t q -> p q t"),
+                factor_turned[:].rearrange("p (q t) -> p q t", t=1).to_broadcast([P, P, PACK]),
                 ALU.mult,
             )
         for h in range(row_tiles):
@@ -286,34 +269,52 @@ def tile_attend_eitherquestion_runcap_keptlarger_kernel(
             nc.vector.quantize_mx(
                 out=w_codes[:, cols].bitcast(FP8X4), scales=w_scales[:, cols], in_=w_bf[h][:].rearrange("p q t -> p (q t)")
             )
-        quantise_values(1)
 
-        for j in range(feat_tiles):
-            cols = slice(j * P, (j + 1) * P)
-            read = bank(2 + j, [P, Q], "read%d" % j)
+        def place(j, rows, b):
+            count = rows.stop - rows.start
+            read = bank(b, [P, count], "read%d_%d" % (j, rows.start))
             nc.tensor.matmul_mx(
                 out=read[:],
-                lhsT=v_codes[:, cols].bitcast(FP8X4),
-                lhsT_scale=v_scales[:, cols],
-                rhs=w_codes[:].bitcast(FP8X4),
-                rhs_scale=w_scales[:],
+                lhsT=v_codes[j].bitcast(FP8X4),
+                lhsT_scale=v_scales[j],
+                rhs=w_codes[:, rows].bitcast(FP8X4),
+                rhs_scale=w_scales[:, rows],
                 start=True,
                 stop=True,
             )
-            read_sb = sb.tile([P, Q], F32, name="read_sb%d" % j, align_bytes=64)
+            read_sb = tile([P, count], F32, "read_sb%d_%d" % (j, rows.start))
             nc.scalar.copy(read_sb[:], read[:])
-            window = windows[j % 2]
-            nc.scalar.activation(window[:].indirect(places[:]), read_sb[:], ACT.Copy)
-            larger = sb.tile([P, M], F32, name="larger%d" % j, align_bytes=64)
-            result = sb.tile([P, M], F32, name="result%d" % j, align_bytes=64)
-            halves = [slice(0, M // 2), slice(M // 2, M)]
-            for cols in halves:
-                nc.vector.tensor_tensor(larger[:, cols], window[:, cols], old_sb[j][:, cols], ALU.max)
-            for cols in halves:
+            nc.scalar.activation(
+                windows[j % 2][:].indirect(places[:, rows.start // 16 : rows.stop // 16]), read_sb[:], ACT.Copy
+            )
+
+        def finish(j):
+            larger = tile([P, M], F32, "larger%d" % j)
+            result = tile([P, M], F32, "result%d" % j)
+            for c in range(2):
+                cols = slice(c * M // 2, (c + 1) * M // 2)
+                nc.vector.tensor_tensor(larger[:, cols], windows[j % 2][:, cols], old_sb[j][:, cols], ALU.max)
+            last = j == feat_tiles - 1
+            pieces = 4 if last else 2
+            for c in range(pieces):
+                cols = slice(c * M // pieces, (c + 1) * M // pieces)
                 nc.vector.scalar_tensor_tensor(
                     result[:, cols], old_sb[j][:, cols], 0.25, larger[:, cols], ALU.mult, ALU.add
                 )
-                if j == feat_tiles - 1:
+                if last:
                     nc.sync.dma_start(out[j * P : (j + 1) * P, cols], result[:, cols])
-            if j < feat_tiles - 1:
+            if not last:
                 nc.sync.dma_start(out[j * P : (j + 1) * P, :], result[:])
+
+        turn_values(2, 1, 1, None, "w_bf0")
+        place(0, slice(0, P), 5)
+        place(0, slice(P, Q), 6)
+        pick_values(3, "w_bf1")
+        place(1, slice(0, Q), 0)
+        finish(0)
+        turn_values(3, 1, 7, "read_sb1_0", "larger0")
+        place(2, slice(0, Q), 2)
+        finish(1)
+        place(3, slice(0, Q), 4)
+        finish(2)
+        finish(3)

from contextlib import ExitStack

import concourse.mybir as mybir
from concourse.masks import make_identity

D, T, I, Q, E, G, M = 512, 2048, 512, 256, 512, 64, 1024
P = 128
PACK = 4
RUN = I // G
QUAD = 32

F32 = mybir.dt.float32
BF16 = mybir.dt.bfloat16
I32 = mybir.dt.int32
U32 = mybir.dt.uint32
U16 = mybir.dt.uint16
U8 = mybir.dt.uint8
FP8X4 = mybir.dt.float8_e4m3fn_x4
ALU = mybir.AluOpType
ACT = mybir.ActivationFunctionType
AX = mybir.AxisListType

FLOPS = 2 * (2 * D * Q * I + I * E * Q)
BYTES = 4 * (2 * D * Q + T + 2 * Q + I + E * T + 2 * E * M) + D * T + (D // 32) * T + 2 * P * (I + Q) // 16


def tile_attend_eitherquestion_runcap_keptlarger_kernel(
    tc, query, query2, keys_words, keys_scales, prior1, lam, cap, slot_factor, vals, old, offs, offs2, out
):
    nc = tc.nc
    slot_tiles = I // P
    row_tiles = Q // P
    feat_tiles = E // P

    with ExitStack() as ctx:
        sb = ctx.enter_context(tc.tile_pool(name="sb", bufs=1))
        ps = ctx.enter_context(tc.psum_pool(name="ps", bufs=1))

        def bank(b, shape, name):
            return ps.tile(shape, F32, tag="bank%d" % b, name=name)

        def tile(shape, dtype, name, buffer=None):
            return sb.tile(shape, dtype, name=name, tag=buffer or name, align_bytes=64)

        slots = sb.tile([P, I // 16], U16, name="slots")
        places = sb.tile([P, Q // 16], U16, name="places")
        scale_pool = tile([P, T], U8, "scale_pool")
        prior_pool = tile([P, T], F32, "prior_pool")
        key_pool = tile([P, T], U32, "key_pool")
        q_raw = [tile([P, PACK, Q], F32, "q_raw%d" % n) for n in range(2)]
        ident = tile([P, P], F32, "ident")

        nc.gpsimd.memset(scale_pool[:].bitcast(I32), 0)
        nc.vector.memset(prior_pool[:].bitcast(I32), 0)
        make_identity(nc, ident[:])
        windows = [tile([P, M], F32, "window%d" % n) for n in range(2)]
        for n in range(2):
            nc.vector.memset(windows[n][:], 0.0)

        nc.sync.dma_start(slots[:], offs)
        nc.sync.dma_start(places[:], offs2)
        for n in range(2):
            nc.sync.dma_start(q_raw[n][:], (query, query2)[n].rearrange("(p t) q -> p t q", t=PACK))
        for quad in range(P // QUAD):
            nc.scalar.dma_start(
                scale_pool[QUAD * quad : QUAD * quad + 4, :].bitcast(I32),
                keys_scales[0, 4 * quad : 4 * quad + 4, :].bitcast(I32),
            )
        nc.scalar.dma_start(prior_pool[0:1, :], prior1[0:1, :])
        nc.sync.dma_start(key_pool[:].bitcast(I32), keys_words[0].rearrange("p n t -> p (n t)").bitcast(I32))

        val_pool = [None] * feat_tiles
        old_sb = [None] * feat_tiles

        def load_values(j, buffer):
            val_pool[j] = tile([P, T], F32, "val_pool%d" % j, buffer)
            nc.sync.dma_start(val_pool[j][:], vals[j * P : (j + 1) * P, :])

        def load_old(j, buffer):
            old_sb[j] = tile([P, M], F32, "old_sb%d" % j, buffer)
            nc.sync.dma_start(old_sb[j][:], old[j * P : (j + 1) * P, :])

        q_codes = tile([P, 2, Q], U32, "q_codes")
        q_scales = tile([P, 2, Q], U8, "q_scales")
        for n in range(2):
            q_bf = tile([P, Q, PACK], BF16, "q_bf%d" % n)
            nc.vector.tensor_copy(
                q_bf[:].rearrange("p (c i) t -> p c t i", i=4),
                q_raw[n][:].rearrange("p t (c i) -> p c t i", i=4),
            )
            nc.vector.quantize_mx(
                out=q_codes[:, n, :].bitcast(FP8X4), scales=q_scales[:, n, :], in_=q_bf[:].rearrange("p q t -> p (q t)")
            )

        key_scales = tile([P, I], U8, "key_scales")
        key_codes = [tile([P, P], U32, "key_codes%d" % j) for j in range(slot_tiles)]
        half = I // 2

        prior_row = tile([P, I], F32, "prior_row")
        nc.scalar.activation(prior_row[:], prior_pool[:].indirect(slots[:]), ACT.Copy)
        prior_ps = bank(7, [P, slot_tiles, P], "prior_ps")
        for j in range(slot_tiles):
            nc.tensor.transpose(prior_ps[:, j, :], prior_row[:, j * P : (j + 1) * P], ident[:])
        row_values = tile([P, P], F32, "row_values", "prior_pool")
        nc.gpsimd.memset(row_values[:], 0.0)
        nc.sync.dma_start(row_values[0:row_tiles, :], lam.rearrange("(h p) o -> h (p o)", p=P))
        nc.sync.dma_start(row_values[QUAD : QUAD + row_tiles, :], cap.rearrange("(h p) o -> h (p o)", p=P))

        nc.vector.tensor_copy(key_scales[:], scale_pool[:].indirect(slots[:]))
        load_values(0, "q_raw1")
        load_values(1, "scale_pool")
        grown = [tile([P, 2, Q], F32, "grown%d" % j) for j in range(slot_tiles)]
        for j in range(slot_tiles):
            nc.vector.tensor_copy(key_codes[j][:], key_pool[:].indirect(slots[:, j * P // 16 : (j + 1) * P // 16]))
            scores = bank(j, [P, 2 * Q], "scores%d" % j)
            nc.tensor.matmul_mx(
                out=scores[:],
                lhsT=key_codes[j][:].bitcast(FP8X4),
                lhsT_scale=key_scales[:, j * P : (j + 1) * P],
                rhs=q_codes[:].rearrange("p n q -> p (n q)").bitcast(FP8X4),
                rhs_scale=q_scales[:].rearrange("p n q -> p (n q)"),
                start=True,
                stop=True,
            )
            nc.scalar.activation(grown[j][:].rearrange("p n q -> p (n q)"), scores[:], ACT.Exp)
        load_values(2, "key_pool")

        prior = [tile([P, slot_tiles], F32, "prior%d" % n) for n in range(2)]
        nc.vector.tensor_copy(prior[0][:], prior_ps[:, :, 0])
        nc.vector.tensor_scalar(prior[1][:], prior_ps[:, :, 0], -1.0, 1.0, ALU.mult, ALU.add)

        mix_banks = [[4, 6], [5, 0]]
        mix = [[bank(mix_banks[h][u], [P, half], "mix%d%d" % (h, u)) for u in range(2)] for h in range(row_tiles)]
        for j in range(slot_tiles):
            terms = [tile([P, Q], F32, "term%d%d" % (j, n)) for n in range(2)]
            for n in range(2):
                nc.vector.tensor_scalar(terms[n][:], grown[j][:, n, :], prior[n][:, j : j + 1], None, ALU.mult)
            for h in range(row_tiles):
                for n in range(2):
                    nc.tensor.matmul(
                        mix[h][j // 2][:, j % 2 * P : (j % 2 + 1) * P],
                        lhsT=terms[n][:, h * P : (h + 1) * P],
                        rhs=ident[:],
                        start=(n == 0),
                        stop=(n == 1),
                        is_transpose=True,
                    )
        factor_sb = tile([P, PACK], F32, "factor_sb", "grown0")
        nc.sync.dma_start(factor_sb[:], slot_factor.rearrange("o (p t) -> p (o t)", t=PACK))
        load_values(3, "term00")


        v_codes = [None] * feat_tiles
        v_scales = [None] * feat_tiles
        picked = [None] * feat_tiles

        def pick_values(j, buffer):
            picked[j] = tile([P, I], BF16, "picked%d" % j, buffer)
            nc.vector.tensor_copy(picked[j][:], val_pool[j][:].indirect(slots[:]))

        def turn_values(first, count, b, bf_buffer, code_buffer):
            v_turned = bank(b, [P, count, 2, P], "v_turned%d" % first)
            for k in range(count):
                words = picked[first + k][:].bitcast(F32)
                for u in range(2):
                    nc.tensor.transpose(v_turned[:, k, u, :], words[:, u : I // 2 : 2], ident[:])
            v_bf = tile([P, count * P * PACK], BF16, "v_bf%d" % first, bf_buffer)
            nc.scalar.copy(
                v_bf[:].bitcast(F32).rearrange("p (k e u) -> p k e u", k=count, u=2),
                v_turned[:].rearrange("p k u e -> p k e u"),
            )
            codes = tile([P, count * P], U32, "v_codes%d" % first, code_buffer)
            scales = tile([P, count * P], U8, "v_scales%d" % first)
            nc.vector.quantize_mx(out=codes[:].bitcast(FP8X4), scales=scales[:], in_=v_bf[:])
            for k in range(count):
                v_codes[first + k] = codes[:, k * P : (k + 1) * P]
                v_scales[first + k] = scales[:, k * P : (k + 1) * P]

        pick_values(0, "grown3")
        load_old(0, "q_raw1")
        pick_values(1, "term31")
        load_old(1, "scale_pool")

        cap_sb = tile([P, row_tiles], F32, "cap_sb")
        logs = [tile([P, PACK, P], F32, "logs%d" % h) for h in range(row_tiles)]
        slot_score = [tile([P, I], F32, "slot_score%d" % h) for h in range(row_tiles)]
        row_max = [tile([P, 1], F32, "row_max%d" % h) for h in range(row_tiles)]
        neg_max = [tile([P, 1], F32, "neg_max%d" % h) for h in range(row_tiles)]
        for h in range(row_tiles):
            for u in range(2):
                nc.scalar.activation(
                    logs[h][:, :, u * P // 2 : (u + 1) * P // 2],
                    mix[h][u][:].rearrange("p (s t) -> p t s", t=PACK),
                    ACT.Ln,
                )
                if h == 0 and u == 0:
                    row_turned = bank(4, [P, P], "row_turned")
                    nc.tensor.transpose(row_turned[:], row_values[:], ident[:])
            nc.vector.tensor_scalar(
                slot_score[h][:],
                logs[h][:].rearrange("p t s -> p (t s)"),
                row_turned[:, h : h + 1],
                None,
                ALU.mult,
                ALU.max,
                accum_out=row_max[h][:],
            )
            if h == 0:
                nc.vector.tensor_copy(cap_sb[:], row_turned[:, QUAD : QUAD + row_tiles])
            nc.vector.tensor_scalar(neg_max[h][:], row_max[h][:], -1.0, None, ALU.mult)
        load_old(2, "logs0")
        pick_values(2, "logs1")
        load_old(3, "key_pool")

        share = [tile([P, I], F32, "share%d" % h) for h in range(row_tiles)]
        row_sum = [tile([P, 1], F32, "row_sum%d" % h) for h in range(row_tiles)]
        cap_sum = [tile([P, 1], F32, "cap_sum%d" % h) for h in range(row_tiles)]
        for h in range(row_tiles):
            nc.scalar.activation(
                share[h][:], slot_score[h][:], ACT.Exp, bias=neg_max[h][:], accum_out=row_sum[h][:]
            )
            nc.scalar.activation(cap_sum[h][:], row_sum[h][:], ACT.Copy, scale=cap_sb[:, h : h + 1])

        turn_values(0, 2, 7, "slot_score1", None)
        scaled = [tile([P, PACK, P], F32, "scaled%d" % h) for h in range(row_tiles)]
        for h in range(row_tiles):
            share_turned = bank(1 + h, [P, PACK, P], "share_turned%d" % h)
            for t in range(PACK):
                nc.tensor.transpose(share_turned[:, t, :], share[h][:, t * P : (t + 1) * P], ident[:])
            for t in range(PACK):
                nc.scalar.activation(scaled[h][:, t, :], share_turned[:, t, :], ACT.Copy, scale=factor_sb[:, t : t + 1])

        run_sum = [tile([P, G], F32, "run_sum%d" % h) for h in range(row_tiles)]
        bound = [tile([P, G], F32, "bound%d" % h) for h in range(row_tiles)]
        inv_bound = [tile([P, G], F32, "inv_bound%d" % h) for h in range(row_tiles)]
        run_factor = [tile([P, P], F32, "run_factor%d" % h) for h in range(row_tiles)]
        for h in range(row_tiles):
            nc.vector.tensor_reduce(
                run_sum[h][:], share[h][:].rearrange("p (t g s) -> p g t s", t=PACK, g=G), AX.XY, ALU.add
            )
        for h in range(row_tiles):
            nc.vector.tensor_scalar(bound[h][:], run_sum[h][:], cap_sum[h][:], None, ALU.max)
        for h in range(row_tiles):
            nc.vector.reciprocal(inv_bound[h][:], bound[h][:])
        for h in range(row_tiles):
            nc.vector.tensor_scalar(
                run_factor[h][:].rearrange("p (g s) -> p g s", g=G),
                inv_bound[h][:].rearrange("p (g s) -> p g s", s=1).to_broadcast([P, G, RUN // PACK]),
                cap_sb[:, h : h + 1],
                None,
                ALU.mult,
            )


        w_codes = tile([P, Q], U32, "w_codes")
        w_scales = tile([P, Q], U8, "w_scales")
        w_bf = [tile([P, P, PACK], BF16, "w_bf%d" % h) for h in range(row_tiles)]
        for h in range(row_tiles):
            factor_turned = bank(3 + h, [P, P], "factor_turned%d" % h)
            nc.tensor.transpose(factor_turned[:], run_factor[h][:], ident[:])
            nc.vector.tensor_tensor(
                w_bf[h][:],
                scaled[h][:].rearrange("p t q -> p q t"),
                factor_turned[:].rearrange("p (q t) -> p q t", t=1).to_broadcast([P, P, PACK]),
                ALU.mult,
            )
        for h in range(row_tiles):
            cols = slice(h * P, (h + 1) * P)
            nc.vector.quantize_mx(
                out=w_codes[:, cols].bitcast(FP8X4), scales=w_scales[:, cols], in_=w_bf[h][:].rearrange("p q t -> p (q t)")
            )

        def place(j, rows, b):
            count = rows.stop - rows.start
            read = bank(b, [P, count], "read%d_%d" % (j, rows.start))
            nc.tensor.matmul_mx(
                out=read[:],
                lhsT=v_codes[j].bitcast(FP8X4),
                lhsT_scale=v_scales[j],
                rhs=w_codes[:, rows].bitcast(FP8X4),
                rhs_scale=w_scales[:, rows],
                start=True,
                stop=True,
            )
            read_sb = tile([P, count], F32, "read_sb%d_%d" % (j, rows.start))
            nc.scalar.copy(read_sb[:], read[:])
            nc.scalar.activation(
                windows[j % 2][:].indirect(places[:, rows.start // 16 : rows.stop // 16]), read_sb[:], ACT.Copy
            )

        def finish(j):
            larger = tile([P, M], F32, "larger%d" % j)
            result = tile([P, M], F32, "result%d" % j)
            for c in range(2):
                cols = slice(c * M // 2, (c + 1) * M // 2)
                nc.vector.tensor_tensor(larger[:, cols], windows[j % 2][:, cols], old_sb[j][:, cols], ALU.max)
            last = j == feat_tiles - 1
            pieces = 4 if last else 2
            for c in range(pieces):
                cols = slice(c * M // pieces, (c + 1) * M // pieces)
                nc.vector.scalar_tensor_tensor(
                    result[:, cols], old_sb[j][:, cols], 0.25, larger[:, cols], ALU.mult, ALU.add
                )
                if last:
                    nc.sync.dma_start(out[j * P : (j + 1) * P, cols], result[:, cols])
            if not last:
                nc.sync.dma_start(out[j * P : (j + 1) * P, :], result[:])

        turn_values(2, 1, 1, None, "w_bf0")
        place(0, slice(0, P), 5)
        place(0, slice(P, Q), 6)
        pick_values(3, "w_bf1")
        place(1, slice(0, Q), 0)
        finish(0)
        turn_values(3, 1, 7, "read_sb1_0", "larger0")
        place(2, slice(0, Q), 2)
        finish(1)
        place(3, slice(0, Q), 4)
        finish(2)
        finish(3)
